import numpy as np
import ml_dtypes


def mxq(x, axis, fmt="e4m3"):
    dtype, down = {"e4m3": (ml_dtypes.float8_e4m3fn, 7), "e5m2": (ml_dtypes.float8_e5m2, 14)}[fmt]
    v = np.moveaxis(np.asarray(x, np.float32).astype(ml_dtypes.bfloat16).astype(np.float64), axis, -1)
    blocks = v.reshape(v.shape[:-1] + (-1, 32))
    amax = np.abs(blocks).max(-1, keepdims=True)
    byte = np.maximum(np.where(amax > 0, np.frexp(amax)[1] - 1 + 127, 0) - down, 1)
    scale = np.exp2(byte - 127.0)
    codes = (blocks / scale).astype(np.float32).astype(dtype).astype(np.float64)
    return np.moveaxis((codes * scale).reshape(v.shape), -1, axis)


WIDE = False


def mx_kscale(k):
    if not WIDE:
        return np.ones(k)
    levels = np.array([10, -10, 5, -5, 0])
    if k % 512:
        return np.exp2(np.random.permutation(np.resize(levels, k // 32))).repeat(32)
    a = np.empty((k // 512, 16))
    for p in range(k // 512):
        a[p, :8] = np.random.permutation(np.resize(levels, 8))
        for g in range(8):
            far = levels[np.abs(levels - a[p, g]) >= 10]
            a[p, g + 8] = far[np.random.randint(len(far))]
    return np.exp2(a.ravel()).repeat(32)


def f64(x):
    return np.asarray(x).astype(np.float64)


def striped(idx):
    return np.tile(idx.reshape(-1, 16).T, (8, 1)).astype(np.uint16)


def unstriped(offs):
    return offs[:16].T.reshape(-1).astype(np.int64)


def pack_weight(w):
    k, n = w.shape
    w = f64(np.asarray(w, np.float32).astype(ml_dtypes.bfloat16)).reshape(k // 32, 32, n)
    amax = np.abs(w).max(1)
    byte = np.clip(np.where(amax > 0, np.frexp(amax)[1] - 1 + 127 - 7, 1), 1, 254)
    scaled = (w * np.exp2(127.0 - byte)[:, None, :]).reshape(k, n).astype(np.float32)
    words = np.ascontiguousarray(scaled.reshape(k // 512, 128, 4, n).transpose(0, 1, 3, 2)).astype(ml_dtypes.float8_e4m3fn).view(np.uint8)
    return words, np.ascontiguousarray(byte.astype(np.uint8).reshape(k // 512, 16, n))


def unpack_weight(words, scales):
    g, p, n, _ = words.shape
    vals = np.ascontiguousarray(words).view(ml_dtypes.float8_e4m3fn).astype(np.float64) * np.repeat(np.exp2(scales.astype(np.float64) - 127.0), 8, axis=1)[..., None]
    return vals.transpose(0, 1, 3, 2).reshape(g * 512, n)


def sigmoid(v):
    return 1.0 / (1.0 + np.exp(-np.maximum(v, -700.0)))


K, T, S, D, H, V, Z, W = 512, 2048, 512, 2, 512, 256, 512, 2048
P = 2 ** 7


def setup_inputs():
    n = np.random.standard_normal
    s = mx_kscale(K)[:, None]
    packed_xT = pack_weight(n((K, T)) * s)
    packed_eT = pack_weight(n((K, W)) * s)
    return {
        "x_words": packed_xT[0],
        "x_scales": packed_xT[1],
        "w1": (n((K, H)) / np.sqrt(K) / s).astype(np.float32),
        "w2": (n((K, H)) / np.sqrt(K) / s).astype(np.float32),
        "e_words": packed_eT[0],
        "e_scales": packed_eT[1],
        "unit": (np.random.uniform(0.6, 1.4, (K, 1)) / np.sqrt(K) / s).astype(np.float32),
        "pop": (np.tile(np.random.uniform(0.3, 1.5, W), (P, 1))).astype(np.float32),
        "offs": striped(np.random.permutation(T)[:S]),
        "itm": striped(np.random.permutation(W)[:Z]),
        "sim": striped(np.random.permutation(V)),
    }


def reference(x_words, x_scales, w1, w2, e_words, e_scales, unit, pop, offs, itm, sim):
    xq = unpack_weight(x_words, x_scales)[:, unstriped(offs)]
    yd = mxq(f64(w2), 0, "e4m3").T @ xq
    att = np.exp(1.1 * np.tanh(yd))
    y = mxq(f64(w1), 0, "e4m3").T @ xq
    ay = att * y
    user = (ay.reshape(len(ay), -1, D).sum(axis=2)) / (att.reshape(len(att), -1, D).sum(axis=2))
    usr2 = user - (0.6 * user[:, unstriped(sim)])
    hid = f64(unit) * usr2
    e_itm = unpack_weight(e_words, e_scales)[:, unstriped(itm)]
    sc = mxq(hid, 0, "e4m3").T @ e_itm
    mu = sc.mean(axis=1, keepdims=True)
    return sigmoid(2.0 * (sc - mu)) - (0.4 * (f64(pop)[:1][:, unstriped(itm)]))

@@ -1,0 +1,217 @@
+from contextlib import ExitStack
+
+import concourse.mybir as mybir
+
+K, T, S, H, V, Z, W = 512, 2048, 512, 512, 256, 512, 2048
+P = 128
+PACK = 4
+FLOPS = 2 * K * H * S * 2 + 2 * H * V * Z
+
+F32 = mybir.dt.float32
+BF16 = mybir.dt.bfloat16
+I32 = mybir.dt.int32
+U32 = mybir.dt.uint32
+U16 = mybir.dt.uint16
+U8 = mybir.dt.uint8
+FP8X4 = mybir.dt.float8_e4m3fn_x4
+ADD = mybir.AluOpType.add
+SUB = mybir.AluOpType.subtract
+MULT = mybir.AluOpType.mult
+SIGMOID = mybir.ActivationFunctionType.Sigmoid
+COPY = mybir.ActivationFunctionType.Copy
+
+
+def tile_picked_yuserst_sig_p_kernel(
+    tc, x_words, x_scales, w1, w2, e_words, e_scales, unit, pop, offs, itm, sim, out
+):
+    nc = tc.nc
+    with ExitStack() as ctx:
+        keep = ctx.enter_context(tc.tile_pool(name="keep", bufs=1))
+        psum = ctx.enter_context(tc.psum_pool(name="psum", bufs=1))
+
+        def tile(shape, dtype, name, over=None):
+            return keep.tile(shape, dtype, name=name, tag=over or name, align_bytes=64)
+
+        offs_sb = keep.tile([P, S // 16], U16, name="offs_sb")
+        itm_sb = keep.tile([P, Z // 16], U16, name="itm_sb")
+        sim_sb = keep.tile([P, V // 16], U16, name="sim_sb")
+        x_table = tile([P, T], U32, "x_table")
+        e_table = tile([P, W], U32, "e_table")
+        x_scale_table = tile([P, T], U8, "x_scale_table")
+        e_scale_table = tile([P, W], U8, "e_scale_table")
+        pop_table = tile([P, W], F32, "pop_table")
+        unit_sb = tile([P, PACK], F32, "unit_sb")
+        half = H // 2
+        w_raw = {
+            (name, h): tile([P, PACK, half], F32, "raw_%s_%d" % (name, h))
+            for name in ("w1", "w2")
+            for h in range(2)
+        }
+
+        def load_words(table, words):
+            nc.sync.dma_start(
+                out=table[:].bitcast(I32),
+                in_=words[0].rearrange("p c r -> p (c r)").bitcast(I32),
+            )
+
+        def load_weight(name, w, h):
+            rows = w.rearrange("(p j) c -> p j c", j=PACK)
+            nc.sync.dma_start(
+                out=w_raw[name, h][:], in_=rows[:, :, h * half : (h + 1) * half]
+            )
+
+        e_plane = tile([P, Z], U8, "e_plane")
+        nc.vector.memset(x_scale_table[:].bitcast(I32), 0)
+        nc.vector.memset(e_scale_table[:].bitcast(I32), 0)
+        nc.vector.memset(e_plane[:].bitcast(I32), 0)
+        nc.sync.dma_start(offs_sb[:], offs)
+        nc.sync.dma_start(itm_sb[:], itm)
+        load_weight("w2", w2, 0)
+        for q in range(4):
+            nc.sync.dma_start(
+                out=x_scale_table[32 * q : 32 * q + 4, :].bitcast(I32),
+                in_=x_scales[0, 4 * q : 4 * q + 4, :].bitcast(I32),
+            )
+        load_weight("w2", w2, 1)
+        nc.sync.dma_start(
+            out=e_scale_table[0:P:8, :].bitcast(I32), in_=e_scales[0].bitcast(I32)
+        )
+        load_words(x_table, x_words)
+        load_weight("w1", w1, 0)
+        load_weight("w1", w1, 1)
+        nc.sync.dma_start(
+            out=unit_sb[:], in_=unit.rearrange("(p t) o -> p (t o)", t=PACK)
+        )
+        nc.sync.dma_start(sim_sb[:], sim)
+        load_words(e_table, e_words)
+        nc.sync.dma_start(out=pop_table[:], in_=pop)
+
+        x_codes = tile([P, S], U32, "x_codes")
+        x_plane = tile([P, S], U8, "x_plane")
+        e_codes = tile([P, Z], U32, "e_codes")
+        e_rows = tile([P, Z], U8, "e_rows")
+        nc.vector.tensor_copy(x_plane[:], x_scale_table[:].indirect(offs_sb[:]))
+        nc.vector.tensor_copy(e_rows[:], e_scale_table[:].indirect(itm_sb[:]))
+        for q in range(4):
+            nc.sync.dma_start(
+                out=e_plane[32 * q : 32 * q + 4, :].bitcast(I32),
+                in_=e_rows[32 * q : 32 * q + 32 : 8, :].bitcast(I32),
+            )
+
+        def quantise_weight(name, copies):
+            grouped = tile([P, PACK, P, PACK], BF16, "grouped_" + name)
+            codes = tile([P, H], U32, "codes_" + name)
+            plane = tile([P, H], U8, "plane_" + name)
+            for h in range(2):
+                ms = slice(h * P // 2, (h + 1) * P // 2)
+                copies[h](
+                    grouped[:, :, ms, :].rearrange("p t m j -> p m t j"),
+                    w_raw[name, h][:].rearrange("p j (m t) -> p m t j", t=PACK),
+                )
+            flat = grouped[:].rearrange("p t m j -> p (t m j)")
+            for lo, hi in ((0, P), (P, H)):
+                nc.vector.quantize_mx(
+                    out=codes[:, lo:hi].bitcast(FP8X4),
+                    scales=plane[:, lo:hi],
+                    in_=flat[:, PACK * lo : PACK * hi],
+                )
+            return codes, plane, grouped
+
+        def product(bank, codes, plane, cols, moving_codes, moving_plane):
+            nc.tensor.matmul_mx(
+                out=bank[:],
+                lhsT=codes[:, cols].bitcast(FP8X4),
+                lhsT_scale=plane[:, cols],
+                rhs=moving_codes[:].bitcast(FP8X4),
+                rhs_scale=moving_plane[:],
+                start=True,
+                stop=True,
+            )
+
+        def pairs(ap):
+            return ap.rearrange("p (v d) -> p d v", d=2)
+
+        w2_codes, w2_plane, w2_grouped = quantise_weight("w2", (nc.scalar.copy, nc.scalar.copy))
+        nc.vector.tensor_copy(x_codes[:], x_table[:].indirect(offs_sb[:]))
+        bounded = []
+        for t in range(PACK):
+            yd = psum.tile([P, S], F32, name="yd", tag="first_%d" % t)
+            product(yd, w2_codes, w2_plane, slice(t * P, (t + 1) * P), x_codes, x_plane)
+            bounded.append(tile([P, 2, V], F32, "bounded_%d" % t))
+            nc.scalar.activation(bounded[t][:], pairs(yd[:]), SIGMOID, scale=2.0)
+
+        w1_codes, w1_plane, w1_grouped = quantise_weight(
+            "w1", (nc.vector.tensor_copy, nc.vector.tensor_copy)
+        )
+        gaps = tile([P, PACK, V], F32, "gaps", over="grouped_w1")
+        share, y, terms, user, alike = {}, {}, {}, {}, {}
+        for t in range(PACK):
+            nc.vector.tensor_tensor(gaps[:, t, :], bounded[t][:, 0, :], bounded[t][:, 1, :], SUB)
+            share[t] = tile([P, 2, V], F32, "share_%d" % t)
+            nc.scalar.activation(share[t][:, 0, :], gaps[:, t, :], SIGMOID, scale=2.2)
+            nc.scalar.activation(share[t][:, 1, :], gaps[:, t, :], SIGMOID, scale=-2.2)
+            y[t] = psum.tile([P, S], F32, name="y", tag="second_%d" % t)
+            product(y[t], w1_codes, w1_plane, slice(t * P, (t + 1) * P), x_codes, x_plane)
+
+        def step_terms(t):
+            terms[t] = tile([P, 2, V], F32, "terms_%d" % t)
+            nc.vector.scalar_tensor_tensor(
+                terms[t][:], pairs(y[t][:]), unit_sb[:, t : t + 1], share[t][:], MULT, MULT
+            )
+
+        def step_user(t):
+            user[t] = tile([P, V], F32, "user_%d" % t)
+            alike[t] = tile([P, V], F32, "alike_%d" % t)
+            nc.vector.tensor_tensor(user[t][:], terms[t][:, 0, :], terms[t][:, 1, :], ADD)
+            for g in range(2):
+                nc.scalar.activation(
+                    alike[t][:, g * P : (g + 1) * P],
+                    user[t][:].indirect(sim_sb[:, g * 8 : (g + 1) * 8]),
+                    COPY,
+                )
+
+        step_terms(0)
+        for t in range(PACK):
+            if t + 1 < PACK:
+                step_terms(t + 1)
+            step_user(t)
+        nc.vector.tensor_copy(e_codes[:], e_table[:].indirect(itm_sb[:]))
+
+        base = tile([P, Z], F32, "base")
+        nc.scalar.activation(base[:], pop_table[:].indirect(itm_sb[:]), COPY, scale=-0.4)
+
+        hid = tile([P, PACK, V], BF16, "hid", over="e_table")
+        for t in range(PACK):
+            nc.vector.scalar_tensor_tensor(hid[:, t, :], alike[t][:], -0.6, user[t][:], MULT, ADD)
+        hid_codes = tile([P, V], U32, "hid_codes")
+        hid_plane = tile([P, V], U8, "hid_plane")
+        groups = []
+        for g, copy in enumerate((nc.vector.tensor_copy, nc.scalar.copy)):
+            grouped = tile([P, P, PACK], BF16, "hid_grouped_%d" % g)
+            copy(grouped[:], hid[:, :, g * P : (g + 1) * P].rearrange("p t v -> p v t"))
+            groups.append(grouped)
+        for g in range(2):
+            vs = slice(g * P, (g + 1) * P)
+            nc.vector.quantize_mx(
+                out=hid_codes[:, vs].bitcast(FP8X4),
+                scales=hid_plane[:, vs],
+                in_=groups[g][:].rearrange("p v t -> p (v t)"),
+            )
+        for g in range(2):
+            vs = slice(g * P, (g + 1) * P)
+            sc = psum.tile([P, Z], F32, name="sc", tag="first_%d" % g)
+            product(sc, hid_codes, hid_plane, vs, e_codes, e_plane)
+            shares = tile([P, Z], F32, "shares_%d" % g)
+            minus_mu = tile([P, 1], F32, "minus_mu_%d" % g)
+            nc.vector.tensor_scalar(
+                shares[:], sc[:], -2.0 / Z, None, MULT, ADD, accum_out=minus_mu[:]
+            )
+            for c in range(2):
+                cols = slice(c * Z // 2, (c + 1) * Z // 2)
+                squashed = tile([P, Z // 2], F32, "squashed_%d_%d" % (g, c))
+                nc.scalar.activation(
+                    squashed[:], shares[:, cols], SIGMOID, scale=-float(Z), bias=minus_mu[:]
+                )
+                result = tile([P, Z // 2], F32, "result_%d_%d" % (g, c))
+                nc.vector.tensor_tensor(result[:], squashed[:], base[:, cols], ADD)
+                nc.sync.dma_start(out=out[vs, cols], in_=result[:])

@@ -88,7 +88,6 @@ def tile_picked_yuserst_sig_p_kernel(
 
         x_codes = tile([P, S], U32, "x_codes")
         x_plane = tile([P, S], U8, "x_plane")
-        e_codes = tile([P, Z], U32, "e_codes")
         e_rows = tile([P, Z], U8, "e_rows")
         nc.vector.tensor_copy(x_plane[:], x_scale_table[:].indirect(offs_sb[:]))
         nc.vector.tensor_copy(e_rows[:], e_scale_table[:].indirect(itm_sb[:]))
@@ -119,11 +118,11 @@ def tile_picked_yuserst_sig_p_kernel(
 
         def product(bank, codes, plane, cols, moving_codes, moving_plane):
             nc.tensor.matmul_mx(
-                out=bank[:],
+                out=bank,
                 lhsT=codes[:, cols].bitcast(FP8X4),
                 lhsT_scale=plane[:, cols],
-                rhs=moving_codes[:].bitcast(FP8X4),
-                rhs_scale=moving_plane[:],
+                rhs=moving_codes.bitcast(FP8X4),
+                rhs_scale=moving_plane,
                 start=True,
                 stop=True,
             )
@@ -132,13 +131,26 @@ def tile_picked_yuserst_sig_p_kernel(
             return ap.rearrange("p (v d) -> p d v", d=2)
 
         w2_codes, w2_plane, w2_grouped = quantise_weight("w2", (nc.scalar.copy, nc.scalar.copy))
-        nc.vector.tensor_copy(x_codes[:], x_table[:].indirect(offs_sb[:]))
-        bounded = []
-        for t in range(PACK):
-            yd = psum.tile([P, S], F32, name="yd", tag="first_%d" % t)
-            product(yd, w2_codes, w2_plane, slice(t * P, (t + 1) * P), x_codes, x_plane)
-            bounded.append(tile([P, 2, V], F32, "bounded_%d" % t))
-            nc.scalar.activation(bounded[t][:], pairs(yd[:]), SIGMOID, scale=2.0)
+        bounded = [tile([P, 2, 2, V], F32, "bounded_%d" % pair) for pair in range(2)]
+        for h in range(2):
+            js = slice(h * S // 2, (h + 1) * S // 2)
+            nc.vector.tensor_copy(
+                x_codes[:, js], x_table[:].indirect(offs_sb[:, h * S // 32 : (h + 1) * S // 32])
+            )
+            for pair in range(2):
+                yd = psum.tile([P, 2, S // 2], F32, name="yd", tag="first_%d" % (2 * h + pair))
+                for u in range(2):
+                    t = 2 * pair + u
+                    product(
+                        yd[:, u, :], w2_codes, w2_plane, slice(t * P, (t + 1) * P),
+                        x_codes[:, js], x_plane[:, js],
+                    )
+                nc.scalar.activation(
+                    bounded[pair][:, :, :, h * V // 2 : (h + 1) * V // 2],
+                    yd[:].rearrange("p u (v d) -> p u d v", d=2),
+                    SIGMOID,
+                    scale=2.0,
+                )
 
         w1_codes, w1_plane, w1_grouped = quantise_weight(
             "w1", (nc.vector.tensor_copy, nc.vector.tensor_copy)
@@ -146,12 +158,15 @@ def tile_picked_yuserst_sig_p_kernel(
         gaps = tile([P, PACK, V], F32, "gaps", over="grouped_w1")
         share, y, terms, user, alike = {}, {}, {}, {}, {}
         for t in range(PACK):
-            nc.vector.tensor_tensor(gaps[:, t, :], bounded[t][:, 0, :], bounded[t][:, 1, :], SUB)
+            both = bounded[t // 2][:, t % 2, :, :]
+            nc.vector.tensor_tensor(gaps[:, t, :], both[:, 0, :], both[:, 1, :], SUB)
             share[t] = tile([P, 2, V], F32, "share_%d" % t)
             nc.scalar.activation(share[t][:, 0, :], gaps[:, t, :], SIGMOID, scale=2.2)
             nc.scalar.activation(share[t][:, 1, :], gaps[:, t, :], SIGMOID, scale=-2.2)
             y[t] = psum.tile([P, S], F32, name="y", tag="second_%d" % t)
-            product(y[t], w1_codes, w1_plane, slice(t * P, (t + 1) * P), x_codes, x_plane)
+            product(
+                y[t][:], w1_codes, w1_plane, slice(t * P, (t + 1) * P), x_codes[:], x_plane[:]
+            )
 
         def step_terms(t):
             terms[t] = tile([P, 2, V], F32, "terms_%d" % t)
@@ -175,21 +190,29 @@ def tile_picked_yuserst_sig_p_kernel(
             if t + 1 < PACK:
                 step_terms(t + 1)
             step_user(t)
-        nc.vector.tensor_copy(e_codes[:], e_table[:].indirect(itm_sb[:]))
+        e_codes = tile([P, Z], U32, "e_codes", over="terms_3")
 
-        base = tile([P, Z], F32, "base")
-        nc.scalar.activation(base[:], pop_table[:].indirect(itm_sb[:]), COPY, scale=-0.4)
+        def pick_items(h):
+            nc.vector.tensor_copy(
+                e_codes[:, h * Z // 2 : (h + 1) * Z // 2],
+                e_table[:].indirect(itm_sb[:, h * Z // 32 : (h + 1) * Z // 32]),
+            )
 
-        hid = tile([P, PACK, V], BF16, "hid", over="e_table")
+        hid = tile([P, PACK, V], BF16, "hid")
         for t in range(PACK):
             nc.vector.scalar_tensor_tensor(hid[:, t, :], alike[t][:], -0.6, user[t][:], MULT, ADD)
         hid_codes = tile([P, V], U32, "hid_codes")
         hid_plane = tile([P, V], U8, "hid_plane")
         groups = []
+        pick_items(0)
         for g, copy in enumerate((nc.vector.tensor_copy, nc.scalar.copy)):
             grouped = tile([P, P, PACK], BF16, "hid_grouped_%d" % g)
             copy(grouped[:], hid[:, :, g * P : (g + 1) * P].rearrange("p t v -> p v t"))
             groups.append(grouped)
+        pick_items(1)
+        base = tile([P, Z], F32, "base", over="hid")
+        nc.scalar.activation(base[:], pop_table[:].indirect(itm_sb[:]), COPY, scale=-0.4)
+
         for g in range(2):
             vs = slice(g * P, (g + 1) * P)
             nc.vector.quantize_mx(
@@ -200,7 +223,7 @@ def tile_picked_yuserst_sig_p_kernel(
         for g in range(2):
             vs = slice(g * P, (g + 1) * P)
             sc = psum.tile([P, Z], F32, name="sc", tag="first_%d" % g)
-            product(sc, hid_codes, hid_plane, vs, e_codes, e_plane)
+            product(sc[:], hid_codes, hid_plane, vs, e_codes[:], e_plane[:])
             shares = tile([P, Z], F32, "shares_%d" % g)
             minus_mu = tile([P, 1], F32, "minus_mu_%d" % g)
             nc.vector.tensor_scalar(

from contextlib import ExitStack

import concourse.mybir as mybir

K, T, S, H, V, Z, W = 512, 2048, 512, 512, 256, 512, 2048
P = 128
PACK = 4
FLOPS = 2 * K * H * S * 2 + 2 * H * V * Z

F32 = mybir.dt.float32
BF16 = mybir.dt.bfloat16
I32 = mybir.dt.int32
U32 = mybir.dt.uint32
U16 = mybir.dt.uint16
U8 = mybir.dt.uint8
FP8X4 = mybir.dt.float8_e4m3fn_x4
ADD = mybir.AluOpType.add
SUB = mybir.AluOpType.subtract
MULT = mybir.AluOpType.mult
SIGMOID = mybir.ActivationFunctionType.Sigmoid
COPY = mybir.ActivationFunctionType.Copy


def tile_picked_yuserst_sig_p_kernel(
    tc, x_words, x_scales, w1, w2, e_words, e_scales, unit, pop, offs, itm, sim, out
):
    nc = tc.nc
    with ExitStack() as ctx:
        keep = ctx.enter_context(tc.tile_pool(name="keep", bufs=1))
        psum = ctx.enter_context(tc.psum_pool(name="psum", bufs=1))

        def tile(shape, dtype, name, over=None):
            return keep.tile(shape, dtype, name=name, tag=over or name, align_bytes=64)

        offs_sb = keep.tile([P, S // 16], U16, name="offs_sb")
        itm_sb = keep.tile([P, Z // 16], U16, name="itm_sb")
        sim_sb = keep.tile([P, V // 16], U16, name="sim_sb")
        x_table = tile([P, T], U32, "x_table")
        e_table = tile([P, W], U32, "e_table")
        x_scale_table = tile([P, T], U8, "x_scale_table")
        e_scale_table = tile([P, W], U8, "e_scale_table")
        pop_table = tile([P, W], F32, "pop_table")
        unit_sb = tile([P, PACK], F32, "unit_sb")
        half = H // 2
        w_raw = {
            (name, h): tile([P, PACK, half], F32, "raw_%s_%d" % (name, h))
            for name in ("w1", "w2")
            for h in range(2)
        }

        def load_words(table, words):
            nc.sync.dma_start(
                out=table[:].bitcast(I32),
                in_=words[0].rearrange("p c r -> p (c r)").bitcast(I32),
            )

        def load_weight(name, w, h):
            rows = w.rearrange("(p j) c -> p j c", j=PACK)
            nc.sync.dma_start(
                out=w_raw[name, h][:], in_=rows[:, :, h * half : (h + 1) * half]
            )

        e_plane = tile([P, Z], U8, "e_plane")
        nc.vector.memset(x_scale_table[:].bitcast(I32), 0)
        nc.vector.memset(e_scale_table[:].bitcast(I32), 0)
        nc.vector.memset(e_plane[:].bitcast(I32), 0)
        nc.sync.dma_start(offs_sb[:], offs)
        nc.sync.dma_start(itm_sb[:], itm)
        load_weight("w2", w2, 0)
        for q in range(4):
            nc.sync.dma_start(
                out=x_scale_table[32 * q : 32 * q + 4, :].bitcast(I32),
                in_=x_scales[0, 4 * q : 4 * q + 4, :].bitcast(I32),
            )
        load_weight("w2", w2, 1)
        nc.sync.dma_start(
            out=e_scale_table[0:P:8, :].bitcast(I32), in_=e_scales[0].bitcast(I32)
        )
        load_words(x_table, x_words)
        load_weight("w1", w1, 0)
        load_weight("w1", w1, 1)
        nc.sync.dma_start(
            out=unit_sb[:], in_=unit.rearrange("(p t) o -> p (t o)", t=PACK)
        )
        nc.sync.dma_start(sim_sb[:], sim)
        load_words(e_table, e_words)
        nc.sync.dma_start(out=pop_table[:], in_=pop)

        x_codes = tile([P, S], U32, "x_codes")
        x_plane = tile([P, S], U8, "x_plane")
        e_rows = tile([P, Z], U8, "e_rows")
        nc.vector.tensor_copy(x_plane[:], x_scale_table[:].indirect(offs_sb[:]))
        nc.vector.tensor_copy(e_rows[:], e_scale_table[:].indirect(itm_sb[:]))
        for q in range(4):
            nc.sync.dma_start(
                out=e_plane[32 * q : 32 * q + 4, :].bitcast(I32),
                in_=e_rows[32 * q : 32 * q + 32 : 8, :].bitcast(I32),
            )

        def quantise_weight(name, copies):
            grouped = tile([P, PACK, P, PACK], BF16, "grouped_" + name)
            codes = tile([P, H], U32, "codes_" + name)
            plane = tile([P, H], U8, "plane_" + name)
            for h in range(2):
                ms = slice(h * P // 2, (h + 1) * P // 2)
                copies[h](
                    grouped[:, :, ms, :].rearrange("p t m j -> p m t j"),
                    w_raw[name, h][:].rearrange("p j (m t) -> p m t j", t=PACK),
                )
            flat = grouped[:].rearrange("p t m j -> p (t m j)")
            for lo, hi in ((0, P), (P, H)):
                nc.vector.quantize_mx(
                    out=codes[:, lo:hi].bitcast(FP8X4),
                    scales=plane[:, lo:hi],
                    in_=flat[:, PACK * lo : PACK * hi],
                )
            return codes, plane, grouped

        def product(bank, codes, plane, cols, moving_codes, moving_plane):
            nc.tensor.matmul_mx(
                out=bank,
                lhsT=codes[:, cols].bitcast(FP8X4),
                lhsT_scale=plane[:, cols],
                rhs=moving_codes.bitcast(FP8X4),
                rhs_scale=moving_plane,
                start=True,
                stop=True,
            )

        def pairs(ap):
            return ap.rearrange("p (v d) -> p d v", d=2)

        w2_codes, w2_plane, w2_grouped = quantise_weight("w2", (nc.scalar.copy, nc.scalar.copy))
        bounded = [tile([P, 2, 2, V], F32, "bounded_%d" % pair) for pair in range(2)]
        for h in range(2):
            js = slice(h * S // 2, (h + 1) * S // 2)
            nc.vector.tensor_copy(
                x_codes[:, js], x_table[:].indirect(offs_sb[:, h * S // 32 : (h + 1) * S // 32])
            )
            for pair in range(2):
                yd = psum.tile([P, 2, S // 2], F32, name="yd", tag="first_%d" % (2 * h + pair))
                for u in range(2):
                    t = 2 * pair + u
                    product(
                        yd[:, u, :], w2_codes, w2_plane, slice(t * P, (t + 1) * P),
                        x_codes[:, js], x_plane[:, js],
                    )
                nc.scalar.activation(
                    bounded[pair][:, :, :, h * V // 2 : (h + 1) * V // 2],
                    yd[:].rearrange("p u (v d) -> p u d v", d=2),
                    SIGMOID,
                    scale=2.0,
                )

        w1_codes, w1_plane, w1_grouped = quantise_weight(
            "w1", (nc.vector.tensor_copy, nc.vector.tensor_copy)
        )
        gaps = tile([P, PACK, V], F32, "gaps", over="grouped_w1")
        share, y, terms, user, alike = {}, {}, {}, {}, {}
        for t in range(PACK):
            both = bounded[t // 2][:, t % 2, :, :]
            nc.vector.tensor_tensor(gaps[:, t, :], both[:, 0, :], both[:, 1, :], SUB)
            share[t] = tile([P, 2, V], F32, "share_%d" % t)
            nc.scalar.activation(share[t][:, 0, :], gaps[:, t, :], SIGMOID, scale=2.2)
            nc.scalar.activation(share[t][:, 1, :], gaps[:, t, :], SIGMOID, scale=-2.2)
            y[t] = psum.tile([P, S], F32, name="y", tag="second_%d" % t)
            product(
                y[t][:], w1_codes, w1_plane, slice(t * P, (t + 1) * P), x_codes[:], x_plane[:]
            )

        def step_terms(t):
            terms[t] = tile([P, 2, V], F32, "terms_%d" % t)
            nc.vector.scalar_tensor_tensor(
                terms[t][:], pairs(y[t][:]), unit_sb[:, t : t + 1], share[t][:], MULT, MULT
            )

        def step_user(t):
            user[t] = tile([P, V], F32, "user_%d" % t)
            alike[t] = tile([P, V], F32, "alike_%d" % t)
            nc.vector.tensor_tensor(user[t][:], terms[t][:, 0, :], terms[t][:, 1, :], ADD)
            for g in range(2):
                nc.scalar.activation(
                    alike[t][:, g * P : (g + 1) * P],
                    user[t][:].indirect(sim_sb[:, g * 8 : (g + 1) * 8]),
                    COPY,
                )

        step_terms(0)
        for t in range(PACK):
            if t + 1 < PACK:
                step_terms(t + 1)
            step_user(t)
        e_codes = tile([P, Z], U32, "e_codes", over="terms_3")

        def pick_items(h):
            nc.vector.tensor_copy(
                e_codes[:, h * Z // 2 : (h + 1) * Z // 2],
                e_table[:].indirect(itm_sb[:, h * Z // 32 : (h + 1) * Z // 32]),
            )

        hid = tile([P, PACK, V], BF16, "hid")
        for t in range(PACK):
            nc.vector.scalar_tensor_tensor(hid[:, t, :], alike[t][:], -0.6, user[t][:], MULT, ADD)
        hid_codes = tile([P, V], U32, "hid_codes")
        hid_plane = tile([P, V], U8, "hid_plane")
        groups = []
        pick_items(0)
        for g, copy in enumerate((nc.vector.tensor_copy, nc.scalar.copy)):
            grouped = tile([P, P, PACK], BF16, "hid_grouped_%d" % g)
            copy(grouped[:], hid[:, :, g * P : (g + 1) * P].rearrange("p t v -> p v t"))
            groups.append(grouped)
        pick_items(1)
        base = tile([P, Z], F32, "base", over="hid")
        nc.scalar.activation(base[:], pop_table[:].indirect(itm_sb[:]), COPY, scale=-0.4)

        for g in range(2):
            vs = slice(g * P, (g + 1) * P)
            nc.vector.quantize_mx(
                out=hid_codes[:, vs].bitcast(FP8X4),
                scales=hid_plane[:, vs],
                in_=groups[g][:].rearrange("p v t -> p (v t)"),
            )
        for g in range(2):
            vs = slice(g * P, (g + 1) * P)
            sc = psum.tile([P, Z], F32, name="sc", tag="first_%d" % g)
            product(sc[:], hid_codes, hid_plane, vs, e_codes[:], e_plane[:])
            shares = tile([P, Z], F32, "shares_%d" % g)
            minus_mu = tile([P, 1], F32, "minus_mu_%d" % g)
            nc.vector.tensor_scalar(
                shares[:], sc[:], -2.0 / Z, None, MULT, ADD, accum_out=minus_mu[:]
            )
            for c in range(2):
                cols = slice(c * Z // 2, (c + 1) * Z // 2)
                squashed = tile([P, Z // 2], F32, "squashed_%d_%d" % (g, c))
                nc.scalar.activation(
                    squashed[:], shares[:, cols], SIGMOID, scale=-float(Z), bias=minus_mu[:]
                )
                result = tile([P, Z // 2], F32, "result_%d_%d" % (g, c))
                nc.vector.tensor_tensor(result[:], squashed[:], base[:, cols], ADD)
                nc.sync.dma_start(out=out[vs, cols], in_=result[:])
